import numpy as np
import ml_dtypes


def mxq(x, axis, fmt="e4m3"):
    dtype, down = {"e4m3": (ml_dtypes.float8_e4m3fn, 7), "e5m2": (ml_dtypes.float8_e5m2, 14)}[fmt]
    v = np.moveaxis(np.asarray(x, np.float32).astype(ml_dtypes.bfloat16).astype(np.float64), axis, -1)
    blocks = v.reshape(v.shape[:-1] + (-1, 32))
    amax = np.abs(blocks).max(-1, keepdims=True)
    byte = np.maximum(np.where(amax > 0, np.frexp(amax)[1] - 1 + 127, 0) - down, 1)
    scale = np.exp2(byte - 127.0)
    codes = (blocks / scale).astype(np.float32).astype(dtype).astype(np.float64)
    return np.moveaxis((codes * scale).reshape(v.shape), -1, axis)


WIDE = False


def mx_kscale(k):
    if not WIDE:
        return np.ones(k)
    levels = np.array([10, -10, 5, -5, 0])
    if k % 512:
        return np.exp2(np.random.permutation(np.resize(levels, k // 32))).repeat(32)
    a = np.empty((k // 512, 16))
    for p in range(k // 512):
        a[p, :8] = np.random.permutation(np.resize(levels, 8))
        for g in range(8):
            far = levels[np.abs(levels - a[p, g]) >= 10]
            a[p, g + 8] = far[np.random.randint(len(far))]
    return np.exp2(a.ravel()).repeat(32)


def f64(x):
    return np.asarray(x).astype(np.float64)


def striped(idx):
    return np.tile(idx.reshape(-1, 16).T, (8, 1)).astype(np.uint16)


def unstriped(offs):
    return offs[:16].T.reshape(-1).astype(np.int64)


E2M1 = np.array([0.0, 0.5, 1.0, 1.5, 2.0, 3.0, 4.0, 6.0, -0.0, -0.5, -1.0, -1.5, -2.0, -3.0, -4.0, -6.0])


def pack_weight(w, fmt):
    k, n = w.shape
    w = f64(np.asarray(w, np.float32).astype(ml_dtypes.bfloat16)).reshape(k // 32, 32, n)
    amax = np.abs(w).max(1)
    if fmt == "e4m3":
        byte = np.frexp(amax)[1] - 1 + 127 - 7
    else:
        mant, ex = np.frexp(amax / 6.0)
        byte = np.where(mant > 0.5, ex, ex - 1) + 127
    byte = np.clip(np.where(amax > 0, byte, 1), 1, 254)
    scaled = (w * np.exp2(127.0 - byte)[:, None, :]).reshape(k, n).astype(np.float32)
    by_word = np.ascontiguousarray(scaled.reshape(k // 512, 128, 4, n).transpose(0, 1, 3, 2))
    if fmt == "e4m3":
        words = by_word.astype(ml_dtypes.float8_e4m3fn).view(np.uint8)
    else:
        c = by_word.astype(ml_dtypes.float4_e2m1fn).view(np.uint8) & 0xF
        words = (c[..., 0::2] | (c[..., 1::2] << 4)).reshape(k // 512, 128, 2 * n)
    return np.ascontiguousarray(words), np.ascontiguousarray(byte.astype(np.uint8).reshape(k // 512, 16, n))


def unpack_weight(words, scales, fmt):
    g, _, n = scales.shape
    words = np.ascontiguousarray(words).reshape(g, 128, n, -1)
    if fmt == "e4m3":
        vals = words.view(ml_dtypes.float8_e4m3fn).astype(np.float64)
    else:
        nib = np.empty((g, 128, n, 4), np.uint8)
        nib[..., 0::2] = words & 0xF
        nib[..., 1::2] = words >> 4
        vals = E2M1[nib]
    vals = vals * np.repeat(np.exp2(scales.astype(np.float64) - 127.0), 8, axis=1)[..., None]
    return vals.transpose(0, 1, 3, 2).reshape(g * 512, n)


def gelu(v):
    return 0.5 * v * (1.0 + np.tanh(np.sqrt(2.0 / np.pi) * (v + 0.044715 * v**3)))


def often(T, S):
    return np.random.permutation(T)[(T * np.random.uniform(0, 1, S) ** 4).astype(np.int64)]


K1, K2, K3, T, S, P, H, N = 1024, 512, 512, 2048, 1024, 512, 1024, 384

def setup_inputs():
    n = np.random.standard_normal
    s1, s2, s3 = mx_kscale(K1)[:, None], mx_kscale(K2)[:, None], mx_kscale(K3)[:, None]
    u = mx_kscale(H)[:, None]
    d = {}
    d["tab_words"], d["tab_scales"] = pack_weight(n((K1, T)) * s1, "e4m3")
    d["tab2_words"], d["tab2_scales"] = pack_weight(n((K2, T)) * s2, "e4m3")
    d["tab3_words"], d["tab3_scales"] = pack_weight(n((K3, T)) * s3, "e4m3")
    d["offs"] = striped(np.random.permutation(T)[:S])
    d["offs2"] = striped(np.random.permutation(T)[:S])
    d["offs3"] = striped(np.random.permutation(T)[:S])
    d["pos1"] = striped(np.random.permutation(S)[:P])
    d["pos2"] = striped(often(S, P))
    d["pos3"] = striped(often(S, P))
    d["w1"] = (n((K1, H)) / s1 / K1**0.5).astype(np.float32)
    d["w2_words"], d["w2_scales"] = pack_weight(n((K2, H)) / s2 / K2**0.5, "e2m1")
    d["w3"] = (n((K3, H)) / s3 * u.T / K3**0.5).astype(np.float32)
    d["b3"] = (0.5 * n(H) * u[:, 0]).astype(np.float32)
    d["notes"] = (0.8 * n((H, P)) * u).astype(np.float32)
    d["w4_words"], d["w4_scales"] = pack_weight(n((H, N)) / u / H**0.5, "e2m1")
    d["w5"] = (n((H, N)) / u / H**0.5).astype(np.float32)
    return d

def reference(tab_words, tab_scales, tab2_words, tab2_scales, tab3_words, tab3_scales, offs, offs2, offs3,
              pos1, pos2, pos3, w1, w2_words, w2_scales, w3, b3, notes, w4_words, w4_scales, w5):
    v = unpack_weight(tab_words, tab_scales, "e4m3")[:, unstriped(offs)]
    v2 = unpack_weight(tab2_words, tab2_scales, "e4m3")[:, unstriped(offs2)]
    v3 = unpack_weight(tab3_words, tab3_scales, "e4m3")[:, unstriped(offs3)]
    a = mxq(f64(w1), 0, "e4m3").T @ v
    b = unpack_weight(w2_words, w2_scales, "e2m1").T @ v2
    d = (mxq(f64(w3), 0, "e4m3").T @ v3) + f64(b3)[:, None]
    x = a[:, unstriped(pos1)] + b[:, unstriped(pos2)]
    dp = d[:, unstriped(pos3)]
    ge = 0.5 * x * (1.0 + np.tanh(0.7978845608028654 * (x + 0.044715 * x**3)))
    z = ge * (dp + f64(notes))
    y1 = unpack_weight(w4_words, w4_scales, "e2m1").T @ mxq(z, 0, "e4m3")
    y2 = mxq(f64(w5), 0, "e4m3").T @ mxq(dp, 0, "e4m3")
    return np.maximum(y1, y2)

@@ -1,0 +1,278 @@
+from contextlib import ExitStack
+
+import concourse.mybir as mybir
+
+K1, K2, K3, T, S, M, H, N = 1024, 512, 512, 2048, 1024, 512, 1024, 384
+FLOPS = 2 * H * S * (K1 + K2 + K3) + 2 * 2 * H * N * M
+
+F32 = mybir.dt.float32
+BF16 = mybir.dt.bfloat16
+I32 = mybir.dt.int32
+U32 = mybir.dt.uint32
+U16 = mybir.dt.uint16
+U8 = mybir.dt.uint8
+E4M3 = mybir.dt.float8_e4m3fn_x4
+E2M1 = mybir.dt.float4_e2m1fn_x4
+ACT = mybir.ActivationFunctionType
+ALU = mybir.AluOpType
+
+P = 128
+PACK = 4
+KP = P * PACK
+BANK = 512
+NT = N // P
+TAIL = 4
+
+
+def tile_list_hop_brew_scores_kernel(
+    tc, tab_words, tab_scales, tab2_words, tab2_scales, tab3_words, tab3_scales, offs, offs2, offs3,
+    pos1, pos2, pos3, w1, w2_words, w2_scales, w3, b3, notes, w4_words, w4_scales, w5, out,
+):
+    nc = tc.nc
+    with ExitStack() as ctx:
+        keep = ctx.enter_context(tc.tile_pool(name="keep", bufs=1))
+        ring = ctx.enter_context(tc.tile_pool(name="ring", bufs=1))
+        psum = ctx.enter_context(tc.psum_pool(name="psum", bufs=1))
+
+        def held(shape, dtype, name):
+            return keep.tile(shape, dtype, name=name, align_bytes=64)
+
+        def load_list(src, name):
+            lst = held([P, src.shape[1]], U16, name)
+            nc.sync.dma_start(lst[:], src)
+            return lst
+
+        def zeroed_plane(width, name):
+            plane = held([P, width], U8, name)
+            nc.vector.memset(plane[:].bitcast(I32), 0)
+            return plane
+
+        def load_stacked_scales(queue, plane, src):
+            passes = src.shape[0]
+            for q in range(4):
+                rows = src[:, 4 * q : 4 * q + 4, :] if passes > 1 else src[0, 4 * q : 4 * q + 4, :]
+                queue.dma_start(plane[32 * q : 32 * q + 4 * passes, :].bitcast(I32), rows.bitcast(I32))
+
+        def load_words(src, name):
+            words = ring.tile([P, T], U32, name=name, tag="table", bufs=3, align_bytes=64)
+            nc.sync.dma_start(words[:].bitcast(I32), src.rearrange("p t i -> p (t i)").bitcast(I32))
+            return words
+
+        def load_raw(src, name):
+            raw = ring.tile([P, PACK, src.shape[1]], F32, name=name, tag="raw", bufs=4, align_bytes=64)
+            nc.sync.dma_start(raw[:], src.rearrange("(p j) c -> p j c", j=PACK))
+            return raw
+
+        def load_notes(g):
+            rows = ring.tile([P, PACK, M], F32, name="notes%d" % g, tag="table", bufs=3, align_bytes=64)
+            nc.sync.dma_start(rows[:], notes[KP * g : KP * (g + 1), :].rearrange("(p t) m -> p t m", t=PACK))
+            return rows
+
+        warm = held([P, 1], F32, "warm")
+        warm_out = held([P, 1], F32, "warm_out")
+        sc3 = zeroed_plane(T, "sc3")
+        nc.vector.memset(warm[:], 0.0)
+        nc.scalar.activation(warm_out[:], warm[:], ACT.Gelu_apprx_tanh)
+        sc2 = zeroed_plane(T, "sc2")
+        sc1 = zeroed_plane(T, "sc1")
+        w2_sc_in = zeroed_plane(H, "w2_sc_in")
+        w4_sc = zeroed_plane(2 * N, "w4_sc")
+
+        w2_in = held([P, 2 * H], U8, "w2_in")
+        nc.sync.dma_start(w2_in[:].bitcast(I32), w2_words[0].bitcast(I32))
+        w3_raw = [load_raw(w3[:, 0:KP], "w3_raw0")]
+        load_stacked_scales(nc.sync, sc3, tab3_scales)
+        offs3_t = load_list(offs3, "offs3_t")
+        tw3 = load_words(tab3_words[0], "tw3")
+        w3_raw.append(load_raw(w3[:, KP:H], "w3_raw1"))
+        b3_t = held([P, 2, PACK], F32, "b3_t")
+        nc.sync.dma_start(b3_t[:], b3.rearrange("(g p t) -> p g t", g=2, t=PACK))
+        load_stacked_scales(nc.sync, sc2, tab2_scales)
+        offs2_t = load_list(offs2, "offs2_t")
+        tw2 = load_words(tab2_words[0], "tw2")
+        pos3_t = load_list(pos3, "pos3_t")
+        load_stacked_scales(nc.sync, w2_sc_in, w2_scales)
+        w1_raw = {}
+        for a in range(2):
+            w1_raw[a, 0] = load_raw(w1[KP * a : KP * (a + 1), 0:KP], "w1_raw%d0" % a)
+        load_stacked_scales(nc.sync, sc1, tab_scales)
+        offs1_t = load_list(offs, "offs1_t")
+        tw1 = [load_words(tab_words[a], "tw1_%d" % a) for a in range(2)]
+        pos1_t = load_list(pos1, "pos1_t")
+        pos2_t = load_list(pos2, "pos2_t")
+        for a in range(2):
+            w1_raw[a, 1] = load_raw(w1[KP * a : KP * (a + 1), KP:H], "w1_raw%d1" % a)
+        s_t = [load_notes(0)]
+        w5_raw = [load_raw(w5[0:KP, :], "w5_raw0")]
+        for q in range(4):
+            nc.sync.dma_start(
+                w4_sc[32 * q : 32 * q + 4, :].bitcast(I32).rearrange("r (a n) -> r a n", a=2),
+                w4_scales[:, 4 * q : 4 * q + 4, :].bitcast(I32).rearrange("a r n -> r a n"))
+        w5_raw.append(load_raw(w5[KP:H, :], "w5_raw1"))
+        s_t.append(load_notes(1))
+        w4_t = held([P, 2, 2 * N], U8, "w4_t")
+        nc.sync.dma_start(w4_t[:].bitcast(I32),
+                          w4_words.bitcast(I32).rearrange("a p n -> p a n"))
+
+        def gather(window, lst, dtype, name):
+            picked = held([P, S], dtype, name)
+            nc.vector.tensor_copy(picked[:], window[:].indirect(lst[:]))
+            return picked
+
+        def staging(width, name):
+            return ring.tile([P, width], BF16, name=name, tag="bf", bufs=3, align_bytes=64)
+
+        def quantise(rounded, name, cuts):
+            width = rounded.shape[1] // PACK
+            codes = held([P, width], U32, name + "_codes")
+            scales = held([P, width], U8, name + "_scales")
+            for c0, c1 in cuts:
+                nc.vector.quantize_mx(out=codes[:, c0:c1].bitcast(E4M3), scales=scales[:, c0:c1],
+                                      in_=rounded[:, PACK * c0 : PACK * c1])
+            return codes, scales
+
+        def quantise_dealt(raw, name):
+            rounded = staging(PACK * KP, name + "_bf")
+            nc.scalar.copy(rounded[:].rearrange("p (t m j) -> p m j t", t=PACK, j=PACK),
+                           raw[:].rearrange("p j (m t) -> p m j t", t=PACK))
+            return quantise(rounded, name, [(0, KP)])
+
+        def quantise_plain(rows, name, cuts):
+            rounded = staging(PACK * rows.shape[2], name + "_bf")
+            nc.scalar.copy(rounded[:].rearrange("p (c i j) -> p c j i", i=4, j=PACK),
+                           rows[:].rearrange("p j (c i) -> p c j i", i=4))
+            return quantise(rounded, name, cuts)
+
+        def first_stage(passes, name, bias=None):
+            rows = ring.tile([P, S], F32, name=name, tag="rows", bufs=12, align_bytes=64)
+            for h in range(S // BANK):
+                cols = slice(BANK * h, BANK * (h + 1))
+                acc = psum.tile([P, BANK], F32, name="acc", tag="acc", bufs=5)
+                for i, (w_codes, w_sc, v_codes, v_sc) in enumerate(passes):
+                    nc.tensor.matmul_mx(out=acc[:], lhsT=w_codes, lhsT_scale=w_sc, rhs=v_codes[:, cols].bitcast(E4M3),
+                                        rhs_scale=v_sc[:, cols], start=(i == 0), stop=(i == len(passes) - 1))
+                if bias is None:
+                    nc.scalar.copy(rows[:, cols], acc[:])
+                else:
+                    nc.scalar.activation(rows[:, cols], acc[:], ACT.Identity, bias=bias)
+            return rows
+
+        def slab(name):
+            return ring.tile([P, PACK, M], F32, name=name, tag="slab", bufs=3, align_bytes=64)
+
+        w2_t = held([P, 2 * H], U8, "w2_t")
+        nc.vector.tensor_copy(w2_t[:].bitcast(U16).rearrange("p (g t m) -> p g t m", g=2, t=PACK),
+                              w2_in[:].bitcast(U16).rearrange("p (g m t) -> p g t m", g=2, t=PACK))
+        v3_sc = gather(sc3, offs3_t, U8, "v3_sc")
+        v3 = gather(tw3, offs3_t, U32, "v3")
+        w3_q = [quantise_dealt(w3_raw[g], "w3_%d" % g) for g in range(2)]
+
+        def tcols(t):
+            return slice(P * t, P * (t + 1))
+
+        def d_rows(g, t):
+            codes, scales = w3_q[g]
+            return first_stage([(codes[:, tcols(t)].bitcast(E4M3), scales[:, tcols(t)], v3, v3_sc)], "d_rows",
+                               bias=b3_t[:, g, t : t + 1])
+
+        def b_rows(g, t):
+            c0 = KP * g + P * t
+            return first_stage([(w2_t[:, 2 * c0 : 2 * (c0 + P)].bitcast(E2M1), w2_sc[:, c0 : c0 + P], v2, v2_sc)], "b_rows")
+
+        def a_rows(g, t):
+            return first_stage([(w1_q[a, g][0][:, tcols(t)].bitcast(E4M3), w1_q[a, g][1][:, tcols(t)], v1[a], v1_sc[4 * a :, :])
+                                for a in range(2)], "a_rows")
+
+        def picked_d(g, rows):
+            dp = slab("dp%d" % g)
+            for t in range(PACK):
+                nc.vector.tensor_copy(dp[:, t, :], rows[t][:].indirect(pos3_t[:]))
+            return dp
+
+        d0 = [d_rows(0, t) for t in range(PACK)]
+        v2_sc = gather(sc2, offs2_t, U8, "v2_sc")
+        v2 = gather(tw2, offs2_t, U32, "v2")
+        w2_sc = held([P, H], U8, "w2_sc")
+        nc.vector.tensor_copy(w2_sc[:].rearrange("p (g t m) -> p g t m", g=2, t=PACK),
+                              w2_sc_in[:].rearrange("p (g m t) -> p g t m", g=2, t=PACK))
+        dp = [picked_d(0, d0)]
+        w1_q = {}
+        for a in range(2):
+            w1_q[a, 0] = quantise_dealt(w1_raw[a, 0], "w1_%d0" % a)
+        v1_sc = gather(sc1, offs1_t, U8, "v1_sc")
+        v1 = [gather(tw1[a], offs1_t, U32, "v1_%d" % a) for a in range(2)]
+        d1 = [d_rows(1, t) for t in range(PACK)]
+        dp.append(picked_d(1, d1))
+
+        def picked_sum(a_t, b_t, cols):
+            width = cols.stop - cols.start
+            lists = slice(cols.start // 16, cols.stop // 16)
+            ap = ring.tile([P, width], F32, name="ap", tag="ap", bufs=2, align_bytes=64)
+            x = ring.tile([P, width], F32, name="x", tag="x", bufs=2, align_bytes=64)
+            nc.vector.tensor_copy(ap[:], a_t[:].indirect(pos1_t[:, lists]))
+            nc.vector.tensor_tensor(x[:], b_t[:].indirect(pos2_t[:, lists]), ap[:], ALU.add)
+            return x
+
+        def add_notes(g):
+            for t in range(PACK):
+                nc.vector.tensor_tensor(s_t[g][:, t, :], dp[g][:, t, :], s_t[g][:, t, :], ALU.add)
+
+        def z_quantised(ge_rows, s_rows, name):
+            rounded = staging(PACK * ge_rows.shape[2], name + "_bf")
+            nc.vector.tensor_tensor(rounded[:].rearrange("p (c i t) -> p c t i", i=4, t=PACK),
+                                    ge_rows.rearrange("p t (c i) -> p c t i", i=4),
+                                    s_rows.rearrange("p t (c i) -> p c t i", i=4), ALU.mult)
+            return quantise(rounded, name, [(0, ge_rows.shape[2])])
+
+        b0 = [b_rows(0, t) for t in range(PACK)]
+        ge0 = slab("ge0")
+        for t in range(PACK):
+            a_t = a_rows(0, t)
+            x = picked_sum(a_t, b0[t], slice(0, M))
+            nc.scalar.activation(ge0[:, t, :], x[:], ACT.Gelu_apprx_tanh)
+            if t < 2:
+                w1_q[t, 1] = quantise_dealt(w1_raw[t, 1], "w1_%d1" % t)
+        add_notes(0)
+        dq = [quantise_plain(dp[0], "dq0", [(0, M)])]
+        zq0 = z_quantised(ge0[:], s_t[0][:], "zq0")
+
+        width = M // TAIL
+        ge1 = slab("ge1")[:].rearrange("p t m -> p (t m)").rearrange("p (c t m) -> p c t m", c=TAIL, t=PACK)
+        w5_q = []
+        y2 = held([P, NT, M], F32, "y2")
+        for t in range(PACK - 1):
+            b_t = b_rows(1, t)
+            a_t = a_rows(1, t)
+            x = picked_sum(a_t, b_t, slice(0, M))
+            nc.scalar.activation(ge1[:, :, t, :], x[:].rearrange("p (c m) -> p c m", c=TAIL), ACT.Gelu_apprx_tanh)
+            if t == 0:
+                add_notes(1)
+                dq.append(quantise_plain(dp[1], "dq1", [(0, M)]))
+                w5_q.append(quantise_plain(w5_raw[0], "w5_0", [(0, 256), (256, N)]))
+            if t == 1:
+                w5_q.append(quantise_plain(w5_raw[1], "w5_1", [(0, 256), (256, N)]))
+        b_t = b_rows(1, PACK - 1)
+        a_t = a_rows(1, PACK - 1)
+        for nt in range(NT):
+            acc = psum.tile([P, M], F32, name="y2_acc", tag="y", bufs=3)
+            for g in range(2):
+                nc.tensor.matmul_mx(out=acc[:], lhsT=w5_q[g][0][:, tcols(nt)].bitcast(E4M3), lhsT_scale=w5_q[g][1][:, tcols(nt)],
+                                    rhs=dq[g][0][:].bitcast(E4M3), rhs_scale=dq[g][1][:], start=(g == 0), stop=(g == 1))
+            nc.scalar.copy(y2[:, nt, :], acc[:])
+
+        out_v = out.rearrange("(nt p) m -> p nt m", p=P)
+        for c in range(TAIL):
+            cols = slice(width * c, width * (c + 1))
+            x = picked_sum(a_t, b_t, cols)
+            nc.scalar.activation(ge1[:, c, PACK - 1, :], x[:], ACT.Gelu_apprx_tanh)
+            zq1 = z_quantised(ge1[:, c, :, :], s_t[1][:, :, cols], "zq1_%d" % c)
+            acc = psum.tile([P, PACK, width], F32, name="y1_acc", tag="y", bufs=3)
+            for nt in range(NT):
+                for g in range(2):
+                    codes, scales = (zq0[0][:, cols], zq0[1][:, cols]) if g == 0 else (zq1[0][:], zq1[1][:])
+                    nc.tensor.matmul_mx(out=acc[:, nt, :], lhsT=w4_t[:, g, 2 * P * nt : 2 * P * (nt + 1)].bitcast(E2M1),
+                                        lhsT_scale=w4_sc[:, N * g + P * nt : N * g + P * (nt + 1)],
+                                        rhs=codes.bitcast(E4M3), rhs_scale=scales, start=(g == 0), stop=(g == 1))
+            res = held([P, NT, width], F32, "res%d" % c)
+            nc.vector.tensor_tensor(res[:], acc[:, 0:NT, :], y2[:, :, cols], ALU.max)
+            nc.sync.dma_start(out_v[:, :, cols], res[:])

@@ -22,6 +22,7 @@ KP = P * PACK
 BANK = 512
 NT = N // P
 TAIL = 4
+LAG = 2
 
 
 def tile_list_hop_brew_scores_kernel(
@@ -54,7 +55,8 @@ def tile_list_hop_brew_scores_kernel(
                 queue.dma_start(plane[32 * q : 32 * q + 4 * passes, :].bitcast(I32), rows.bitcast(I32))
 
         def load_words(src, name):
-            words = ring.tile([P, T], U32, name=name, tag="table", bufs=3, align_bytes=64)
+            tag, bufs = ("late", 1) if name == "tw1_1" else ("table", 3)
+            words = ring.tile([P, T], U32, name=name, tag=tag, bufs=bufs, align_bytes=64)
             nc.sync.dma_start(words[:].bitcast(I32), src.rearrange("p t i -> p (t i)").bitcast(I32))
             return words
 
@@ -72,43 +74,42 @@ def tile_list_hop_brew_scores_kernel(
         warm_out = held([P, 1], F32, "warm_out")
         sc3 = zeroed_plane(T, "sc3")
         nc.vector.memset(warm[:], 0.0)
-        nc.scalar.activation(warm_out[:], warm[:], ACT.Gelu_apprx_tanh)
         sc2 = zeroed_plane(T, "sc2")
         sc1 = zeroed_plane(T, "sc1")
         w2_sc_in = zeroed_plane(H, "w2_sc_in")
         w4_sc = zeroed_plane(2 * N, "w4_sc")
 
-        w2_in = held([P, 2 * H], U8, "w2_in")
-        nc.sync.dma_start(w2_in[:].bitcast(I32), w2_words[0].bitcast(I32))
-        w3_raw = [load_raw(w3[:, 0:KP], "w3_raw0")]
-        load_stacked_scales(nc.sync, sc3, tab3_scales)
         offs3_t = load_list(offs3, "offs3_t")
+        load_stacked_scales(nc.scalar, sc3, tab3_scales)
+        load_stacked_scales(nc.scalar, sc2, tab2_scales)
+        nc.scalar.activation(warm_out[:], warm[:], ACT.Gelu_apprx_tanh)
+        w3_raw = [load_raw(w3[:, 0:KP], "w3_raw0")]
         tw3 = load_words(tab3_words[0], "tw3")
-        w3_raw.append(load_raw(w3[:, KP:H], "w3_raw1"))
         b3_t = held([P, 2, PACK], F32, "b3_t")
-        nc.sync.dma_start(b3_t[:], b3.rearrange("(g p t) -> p g t", g=2, t=PACK))
-        load_stacked_scales(nc.sync, sc2, tab2_scales)
+        nc.gpsimd.dma_start(b3_t[:], b3.rearrange("(g p t) -> p g t", g=2, t=PACK))
+        load_stacked_scales(nc.gpsimd, sc1, tab_scales)
+        for q in range(4):
+            nc.gpsimd.dma_start(
+                w4_sc[32 * q : 32 * q + 4, :].bitcast(I32).rearrange("r (a n) -> r a n", a=2),
+                w4_scales[:, 4 * q : 4 * q + 4, :].bitcast(I32).rearrange("a r n -> r a n"))
+        w3_raw.append(load_raw(w3[:, KP:H], "w3_raw1"))
         offs2_t = load_list(offs2, "offs2_t")
+        offs1_t = load_list(offs, "offs1_t")
         tw2 = load_words(tab2_words[0], "tw2")
         pos3_t = load_list(pos3, "pos3_t")
-        load_stacked_scales(nc.sync, w2_sc_in, w2_scales)
+        w2_in = held([P, 2 * H], U8, "w2_in")
+        nc.sync.dma_start(w2_in[:].bitcast(I32), w2_words[0].bitcast(I32))
         w1_raw = {}
-        for a in range(2):
-            w1_raw[a, 0] = load_raw(w1[KP * a : KP * (a + 1), 0:KP], "w1_raw%d0" % a)
-        load_stacked_scales(nc.sync, sc1, tab_scales)
-        offs1_t = load_list(offs, "offs1_t")
+        w1_raw[0, 0] = load_raw(w1[0:KP, 0:KP], "w1_raw00")
+        w1_raw[1, 0] = load_raw(w1[KP:K1, 0:KP], "w1_raw10")
+        load_stacked_scales(nc.sync, w2_sc_in, w2_scales)
         tw1 = [load_words(tab_words[a], "tw1_%d" % a) for a in range(2)]
         pos1_t = load_list(pos1, "pos1_t")
         pos2_t = load_list(pos2, "pos2_t")
         for a in range(2):
             w1_raw[a, 1] = load_raw(w1[KP * a : KP * (a + 1), KP:H], "w1_raw%d1" % a)
         s_t = [load_notes(0)]
-        w5_raw = [load_raw(w5[0:KP, :], "w5_raw0")]
-        for q in range(4):
-            nc.sync.dma_start(
-                w4_sc[32 * q : 32 * q + 4, :].bitcast(I32).rearrange("r (a n) -> r a n", a=2),
-                w4_scales[:, 4 * q : 4 * q + 4, :].bitcast(I32).rearrange("a r n -> r a n"))
-        w5_raw.append(load_raw(w5[KP:H, :], "w5_raw1"))
+        w5_raw = [load_raw(w5[KP * g : KP * (g + 1), :], "w5_raw%d" % g) for g in range(2)]
         s_t.append(load_notes(1))
         w4_t = held([P, 2, 2 * N], U8, "w4_t")
         nc.sync.dma_start(w4_t[:].bitcast(I32),
@@ -158,11 +159,10 @@ def tile_list_hop_brew_scores_kernel(
             return rows
 
         def slab(name):
-            return ring.tile([P, PACK, M], F32, name=name, tag="slab", bufs=3, align_bytes=64)
+            if name == "dp1":
+                return ring.tile([P, PACK, M], F32, name=name, tag="late", bufs=1, align_bytes=64)
+            return ring.tile([P, PACK, M], F32, name=name, tag="slab", bufs=2, align_bytes=64)
 
-        w2_t = held([P, 2 * H], U8, "w2_t")
-        nc.vector.tensor_copy(w2_t[:].bitcast(U16).rearrange("p (g t m) -> p g t m", g=2, t=PACK),
-                              w2_in[:].bitcast(U16).rearrange("p (g m t) -> p g t m", g=2, t=PACK))
         v3_sc = gather(sc3, offs3_t, U8, "v3_sc")
         v3 = gather(tw3, offs3_t, U32, "v3")
         w3_q = [quantise_dealt(w3_raw[g], "w3_%d" % g) for g in range(2)]
@@ -192,6 +192,9 @@ def tile_list_hop_brew_scores_kernel(
         d0 = [d_rows(0, t) for t in range(PACK)]
         v2_sc = gather(sc2, offs2_t, U8, "v2_sc")
         v2 = gather(tw2, offs2_t, U32, "v2")
+        w2_t = held([P, 2 * H], U8, "w2_t")
+        nc.vector.tensor_copy(w2_t[:].bitcast(U16).rearrange("p (g t m) -> p g t m", g=2, t=PACK),
+                              w2_in[:].bitcast(U16).rearrange("p (g m t) -> p g t m", g=2, t=PACK))
         w2_sc = held([P, H], U8, "w2_sc")
         nc.vector.tensor_copy(w2_sc[:].rearrange("p (g t m) -> p g t m", g=2, t=PACK),
                               w2_sc_in[:].rearrange("p (g m t) -> p g t m", g=2, t=PACK))
@@ -207,15 +210,15 @@ def tile_list_hop_brew_scores_kernel(
         def picked_sum(a_t, b_t, cols):
             width = cols.stop - cols.start
             lists = slice(cols.start // 16, cols.stop // 16)
-            ap = ring.tile([P, width], F32, name="ap", tag="ap", bufs=2, align_bytes=64)
-            x = ring.tile([P, width], F32, name="x", tag="x", bufs=2, align_bytes=64)
+            ap = ring.tile([P, width], F32, name="ap", tag="ap", bufs=3, align_bytes=64)
+            x = ring.tile([P, width], F32, name="x", tag="x", bufs=5, align_bytes=64)
             nc.vector.tensor_copy(ap[:], a_t[:].indirect(pos1_t[:, lists]))
             nc.vector.tensor_tensor(x[:], b_t[:].indirect(pos2_t[:, lists]), ap[:], ALU.add)
             return x
 
         def add_notes(g):
             for t in range(PACK):
-                nc.vector.tensor_tensor(s_t[g][:, t, :], dp[g][:, t, :], s_t[g][:, t, :], ALU.add)
+                nc.gpsimd.tensor_tensor(s_t[g][:, t, :], dp[g][:, t, :], s_t[g][:, t, :], ALU.add)
 
         def z_quantised(ge_rows, s_rows, name):
             rounded = staging(PACK * ge_rows.shape[2], name + "_bf")
@@ -224,46 +227,59 @@ def tile_list_hop_brew_scores_kernel(
                                     s_rows.rearrange("p t (c i) -> p c t i", i=4), ALU.mult)
             return quantise(rounded, name, [(0, ge_rows.shape[2])])
 
-        b0 = [b_rows(0, t) for t in range(PACK)]
-        ge0 = slab("ge0")
-        for t in range(PACK):
-            a_t = a_rows(0, t)
-            x = picked_sum(a_t, b0[t], slice(0, M))
-            nc.scalar.activation(ge0[:, t, :], x[:], ACT.Gelu_apprx_tanh)
-            if t < 2:
-                w1_q[t, 1] = quantise_dealt(w1_raw[t, 1], "w1_%d1" % t)
-        add_notes(0)
-        dq = [quantise_plain(dp[0], "dq0", [(0, M)])]
-        zq0 = z_quantised(ge0[:], s_t[0][:], "zq0")
-
         width = M // TAIL
+        b_t = [b_rows(0, t) for t in range(PACK)]
+        ge0 = slab("ge0")
         ge1 = slab("ge1")[:].rearrange("p t m -> p (t m)").rearrange("p (c t m) -> p c t m", c=TAIL, t=PACK)
-        w5_q = []
         y2 = held([P, NT, M], F32, "y2")
-        for t in range(PACK - 1):
-            b_t = b_rows(1, t)
-            a_t = a_rows(1, t)
-            x = picked_sum(a_t, b_t, slice(0, M))
-            nc.scalar.activation(ge1[:, :, t, :], x[:].rearrange("p (c m) -> p c m", c=TAIL), ACT.Gelu_apprx_tanh)
-            if t == 0:
+        dq, w5_q, xs = [], [], []
+
+        def gelu(i):
+            if i < PACK:
+                nc.scalar.activation(ge0[:, i, :], xs[i][:], ACT.Gelu_apprx_tanh)
+            else:
+                nc.scalar.activation(ge1[:, :, i - PACK, :], xs[i][:].rearrange("p (c m) -> p c m", c=TAIL), ACT.Gelu_apprx_tanh)
+
+        def kettle_scores():
+            for nt in range(NT):
+                acc = psum.tile([P, M], F32, name="y2_acc", tag="y", bufs=3)
+                for g in range(2):
+                    nc.tensor.matmul_mx(out=acc[:], lhsT=w5_q[g][0][:, tcols(nt)].bitcast(E4M3), lhsT_scale=w5_q[g][1][:, tcols(nt)],
+                                        rhs=dq[g][0][:].bitcast(E4M3), rhs_scale=dq[g][1][:], start=(g == 0), stop=(g == 1))
+                nc.scalar.copy(y2[:, nt, :], acc[:])
+
+        last = 2 * PACK - 1
+        for i in range(2 * PACK):
+            g, t = divmod(i, PACK)
+            if g == 1:
+                b_t.append(b_rows(g, t))
+            a_t = a_rows(g, t)
+            if i < last:
+                xs.append(picked_sum(a_t, b_t[i], slice(0, M)))
+            if i >= LAG:
+                gelu(i - LAG)
+            if i < 2:
+                w1_q[i, 1] = quantise_dealt(w1_raw[i, 1], "w1_%d1" % i)
+            if i == 2:
+                add_notes(0)
+                dq.append(quantise_plain(dp[0], "dq0", [(0, M)]))
+            if i == 3:
+                w5_q.append(quantise_plain(w5_raw[0], "w5_0", [(0, 256), (256, N)]))
+            if i == 4:
                 add_notes(1)
                 dq.append(quantise_plain(dp[1], "dq1", [(0, M)]))
-                w5_q.append(quantise_plain(w5_raw[0], "w5_0", [(0, 256), (256, N)]))
-            if t == 1:
+            if i == 5:
                 w5_q.append(quantise_plain(w5_raw[1], "w5_1", [(0, 256), (256, N)]))
-        b_t = b_rows(1, PACK - 1)
-        a_t = a_rows(1, PACK - 1)
-        for nt in range(NT):
-            acc = psum.tile([P, M], F32, name="y2_acc", tag="y", bufs=3)
-            for g in range(2):
-                nc.tensor.matmul_mx(out=acc[:], lhsT=w5_q[g][0][:, tcols(nt)].bitcast(E4M3), lhsT_scale=w5_q[g][1][:, tcols(nt)],
-                                    rhs=dq[g][0][:].bitcast(E4M3), rhs_scale=dq[g][1][:], start=(g == 0), stop=(g == 1))
-            nc.scalar.copy(y2[:, nt, :], acc[:])
+            if i == PACK - 1 + LAG:
+                zq0 = z_quantised(ge0[:], s_t[0][:], "zq0")
+        kettle_scores()
+        for i in range(2 * PACK - LAG, last):
+            gelu(i)
 
         out_v = out.rearrange("(nt p) m -> p nt m", p=P)
         for c in range(TAIL):
             cols = slice(width * c, width * (c + 1))
-            x = picked_sum(a_t, b_t, cols)
+            x = picked_sum(a_t, b_t[last], cols)
             nc.scalar.activation(ge1[:, c, PACK - 1, :], x[:], ACT.Gelu_apprx_tanh)
             zq1 = z_quantised(ge1[:, c, :, :], s_t[1][:, :, cols], "zq1_%d" % c)
             acc = psum.tile([P, PACK, width], F32, name="y1_acc", tag="y", bufs=3)

@@ -22,7 +22,8 @@ KP = P * PACK
 BANK = 512
 NT = N // P
 TAIL = 4
-LAG = 2
+LAG = 3
+GP = ("w5_0", "w5_1")
 
 
 def tile_list_hop_brew_scores_kernel(
@@ -72,19 +73,19 @@ def tile_list_hop_brew_scores_kernel(
 
         warm = held([P, 1], F32, "warm")
         warm_out = held([P, 1], F32, "warm_out")
-        sc3 = zeroed_plane(T, "sc3")
         nc.vector.memset(warm[:], 0.0)
+        nc.scalar.activation(warm_out[:], warm[:], ACT.Gelu_apprx_tanh)
+        sc3 = zeroed_plane(T, "sc3")
         sc2 = zeroed_plane(T, "sc2")
         sc1 = zeroed_plane(T, "sc1")
         w2_sc_in = zeroed_plane(H, "w2_sc_in")
         w4_sc = zeroed_plane(2 * N, "w4_sc")
 
+        tw3 = load_words(tab3_words[0], "tw3")
         offs3_t = load_list(offs3, "offs3_t")
         load_stacked_scales(nc.scalar, sc3, tab3_scales)
         load_stacked_scales(nc.scalar, sc2, tab2_scales)
-        nc.scalar.activation(warm_out[:], warm[:], ACT.Gelu_apprx_tanh)
         w3_raw = [load_raw(w3[:, 0:KP], "w3_raw0")]
-        tw3 = load_words(tab3_words[0], "tw3")
         b3_t = held([P, 2, PACK], F32, "b3_t")
         nc.gpsimd.dma_start(b3_t[:], b3.rearrange("(g p t) -> p g t", g=2, t=PACK))
         load_stacked_scales(nc.gpsimd, sc1, tab_scales)
@@ -106,11 +107,13 @@ def tile_list_hop_brew_scores_kernel(
         tw1 = [load_words(tab_words[a], "tw1_%d" % a) for a in range(2)]
         pos1_t = load_list(pos1, "pos1_t")
         pos2_t = load_list(pos2, "pos2_t")
-        for a in range(2):
-            w1_raw[a, 1] = load_raw(w1[KP * a : KP * (a + 1), KP:H], "w1_raw%d1" % a)
-        s_t = [load_notes(0)]
-        w5_raw = [load_raw(w5[KP * g : KP * (g + 1), :], "w5_raw%d" % g) for g in range(2)]
-        s_t.append(load_notes(1))
+        s_t, w5_raw = [], []
+        w1_raw[0, 1] = load_raw(w1[0:KP, KP:H], "w1_raw01")
+        w1_raw[1, 1] = load_raw(w1[KP:K1, KP:H], "w1_raw11")
+        s_t.append(load_notes(len(s_t)))
+        s_t.append(load_notes(len(s_t)))
+        w5_raw.append(load_raw(w5[KP * len(w5_raw) : KP * (len(w5_raw) + 1), :], "w5_raw%d" % len(w5_raw)))
+        w5_raw.append(load_raw(w5[KP * len(w5_raw) : KP * (len(w5_raw) + 1), :], "w5_raw%d" % len(w5_raw)))
         w4_t = held([P, 2, 2 * N], U8, "w4_t")
         nc.sync.dma_start(w4_t[:].bitcast(I32),
                           w4_words.bitcast(I32).rearrange("a p n -> p a n"))
@@ -139,13 +142,20 @@ def tile_list_hop_brew_scores_kernel(
             return quantise(rounded, name, [(0, KP)])
 
         def quantise_plain(rows, name, cuts):
+            if name in GP:
+                rounded = ring.tile([P, PACK * rows.shape[2]], BF16, name=name + "_bf", tag="gbf", bufs=2, align_bytes=64)
+                half = rows.shape[2] // 2
+                for c0 in (0, half):
+                    nc.gpsimd.tensor_scalar(rounded[:, PACK * c0 : PACK * (c0 + half)].rearrange("p (c j) -> p c j", j=PACK),
+                                            rows[:, :, c0 : c0 + half].rearrange("p j c -> p c j"), 1.0, 0.0, ALU.mult, ALU.add)
+                return quantise(rounded, name, cuts)
             rounded = staging(PACK * rows.shape[2], name + "_bf")
             nc.scalar.copy(rounded[:].rearrange("p (c i j) -> p c j i", i=4, j=PACK),
                            rows[:].rearrange("p j (c i) -> p c j i", i=4))
             return quantise(rounded, name, cuts)
 
         def first_stage(passes, name, bias=None):
-            rows = ring.tile([P, S], F32, name=name, tag="rows", bufs=12, align_bytes=64)
+            rows = ring.tile([P, S], F32, name=name, tag="rows", bufs=10, align_bytes=64)
             for h in range(S // BANK):
                 cols = slice(BANK * h, BANK * (h + 1))
                 acc = psum.tile([P, BANK], F32, name="acc", tag="acc", bufs=5)
@@ -163,8 +173,8 @@ def tile_list_hop_brew_scores_kernel(
                 return ring.tile([P, PACK, M], F32, name=name, tag="late", bufs=1, align_bytes=64)
             return ring.tile([P, PACK, M], F32, name=name, tag="slab", bufs=2, align_bytes=64)
 
-        v3_sc = gather(sc3, offs3_t, U8, "v3_sc")
         v3 = gather(tw3, offs3_t, U32, "v3")
+        v3_sc = gather(sc3, offs3_t, U8, "v3_sc")
         w3_q = [quantise_dealt(w3_raw[g], "w3_%d" % g) for g in range(2)]
 
         def tcols(t):
@@ -207,13 +217,14 @@ def tile_list_hop_brew_scores_kernel(
         d1 = [d_rows(1, t) for t in range(PACK)]
         dp.append(picked_d(1, d1))
 
-        def picked_sum(a_t, b_t, cols):
-            width = cols.stop - cols.start
-            lists = slice(cols.start // 16, cols.stop // 16)
-            ap = ring.tile([P, width], F32, name="ap", tag="ap", bufs=3, align_bytes=64)
-            x = ring.tile([P, width], F32, name="x", tag="x", bufs=5, align_bytes=64)
-            nc.vector.tensor_copy(ap[:], a_t[:].indirect(pos1_t[:, lists]))
-            nc.vector.tensor_tensor(x[:], b_t[:].indirect(pos2_t[:, lists]), ap[:], ALU.add)
+        def picked_b(rows, cols):
+            bp = ring.tile([P, cols.stop - cols.start], F32, name="bp", tag="bp", bufs=6, align_bytes=64)
+            nc.vector.tensor_copy(bp[:], rows[:].indirect(pos2_t[:, cols.start // 16 : cols.stop // 16]))
+            return bp
+
+        def picked_sum(rows, bp, cols):
+            x = ring.tile([P, cols.stop - cols.start], F32, name="x", tag="x", bufs=5, align_bytes=64)
+            nc.vector.tensor_tensor(x[:], rows[:].indirect(pos1_t[:, cols.start // 16 : cols.stop // 16]), bp[:, cols], ALU.add)
             return x
 
         def add_notes(g):
@@ -228,7 +239,7 @@ def tile_list_hop_brew_scores_kernel(
             return quantise(rounded, name, [(0, ge_rows.shape[2])])
 
         width = M // TAIL
-        b_t = [b_rows(0, t) for t in range(PACK)]
+        b_t = [picked_b(b_rows(0, t), slice(0, M)) for t in range(4)]
         ge0 = slab("ge0")
         ge1 = slab("ge1")[:].rearrange("p t m -> p (t m)").rearrange("p (c t m) -> p c t m", c=TAIL, t=PACK)
         y2 = held([P, NT, M], F32, "y2")
@@ -248,11 +259,15 @@ def tile_list_hop_brew_scores_kernel(
                                         rhs=dq[g][0][:].bitcast(E4M3), rhs_scale=dq[g][1][:], start=(g == 0), stop=(g == 1))
                 nc.scalar.copy(y2[:, nt, :], acc[:])
 
+        add_notes(0)
+        for g in range(2):
+            w5_q.append(quantise_plain(w5_raw[g], "w5_%d" % g, [(0, 256), (256, N)]))
+        add_notes(1)
         last = 2 * PACK - 1
         for i in range(2 * PACK):
             g, t = divmod(i, PACK)
-            if g == 1:
-                b_t.append(b_rows(g, t))
+            if len(b_t) < 2 * PACK and i >= 0:
+                b_t.append(picked_b(b_rows(*divmod(len(b_t), PACK)), slice(0, M)))
             a_t = a_rows(g, t)
             if i < last:
                 xs.append(picked_sum(a_t, b_t[i], slice(0, M)))
@@ -261,15 +276,9 @@ def tile_list_hop_brew_scores_kernel(
             if i < 2:
                 w1_q[i, 1] = quantise_dealt(w1_raw[i, 1], "w1_%d1" % i)
             if i == 2:
-                add_notes(0)
                 dq.append(quantise_plain(dp[0], "dq0", [(0, M)]))
-            if i == 3:
-                w5_q.append(quantise_plain(w5_raw[0], "w5_0", [(0, 256), (256, N)]))
             if i == 4:
-                add_notes(1)
                 dq.append(quantise_plain(dp[1], "dq1", [(0, M)]))
-            if i == 5:
-                w5_q.append(quantise_plain(w5_raw[1], "w5_1", [(0, 256), (256, N)]))
             if i == PACK - 1 + LAG:
                 zq0 = z_quantised(ge0[:], s_t[0][:], "zq0")
         kettle_scores()

@@ -142,16 +142,10 @@ def tile_list_hop_brew_scores_kernel(
             return quantise(rounded, name, [(0, KP)])
 
         def quantise_plain(rows, name, cuts):
-            if name in GP:
-                rounded = ring.tile([P, PACK * rows.shape[2]], BF16, name=name + "_bf", tag="gbf", bufs=2, align_bytes=64)
-                half = rows.shape[2] // 2
-                for c0 in (0, half):
-                    nc.gpsimd.tensor_scalar(rounded[:, PACK * c0 : PACK * (c0 + half)].rearrange("p (c j) -> p c j", j=PACK),
-                                            rows[:, :, c0 : c0 + half].rearrange("p j c -> p c j"), 1.0, 0.0, ALU.mult, ALU.add)
-                return quantise(rounded, name, cuts)
             rounded = staging(PACK * rows.shape[2], name + "_bf")
-            nc.scalar.copy(rounded[:].rearrange("p (c i j) -> p c j i", i=4, j=PACK),
-                           rows[:].rearrange("p j (c i) -> p c j i", i=4))
+            copy = nc.vector.tensor_copy if name in GP else nc.scalar.copy
+            copy(rounded[:].rearrange("p (c i j) -> p c j i", i=4, j=PACK),
+                 rows[:].rearrange("p j (c i) -> p c j i", i=4))
             return quantise(rounded, name, cuts)
 
         def first_stage(passes, name, bias=None):
@@ -260,8 +254,6 @@ def tile_list_hop_brew_scores_kernel(
                 nc.scalar.copy(y2[:, nt, :], acc[:])
 
         add_notes(0)
-        for g in range(2):
-            w5_q.append(quantise_plain(w5_raw[g], "w5_%d" % g, [(0, 256), (256, N)]))
         add_notes(1)
         last = 2 * PACK - 1
         for i in range(2 * PACK):
@@ -277,8 +269,10 @@ def tile_list_hop_brew_scores_kernel(
                 w1_q[i, 1] = quantise_dealt(w1_raw[i, 1], "w1_%d1" % i)
             if i == 2:
                 dq.append(quantise_plain(dp[0], "dq0", [(0, M)]))
-            if i == 4:
+            if i == 3:
                 dq.append(quantise_plain(dp[1], "dq1", [(0, M)]))
+            if i in (4, 5):
+                w5_q.append(quantise_plain(w5_raw[len(w5_q)], "w5_%d" % len(w5_q), [(0, 256), (256, N)]))
             if i == PACK - 1 + LAG:
                 zq0 = z_quantised(ge0[:], s_t[0][:], "zq0")
         kettle_scores()

@@ -19,11 +19,25 @@ ALU = mybir.AluOpType
 P = 128
 PACK = 4
 KP = P * PACK
+GROUPS = H // KP
+TILES = GROUPS * PACK
+QUADS = 4
 BANK = 512
 NT = N // P
-TAIL = 4
+CHUNK = 128
+CHUNKS = M // CHUNK
 LAG = 3
-GP = ("w5_0", "w5_1")
+W5_CUTS = [(0, 256), (256, N)]
+
+TABLE_BUFS = 3
+RAW_BUFS = 4
+STAGE_BUFS = 3
+ROW_BUFS = 10
+GROUP_BUFS = 2
+PICKED_B_BUFS = PACK + 2
+SUM_BUFS = LAG + 2
+ACC_BANKS = 5
+Y2_BANKS = NT
 
 
 def tile_list_hop_brew_scores_kernel(
@@ -39,6 +53,9 @@ def tile_list_hop_brew_scores_kernel(
         def held(shape, dtype, name):
             return keep.tile(shape, dtype, name=name, align_bytes=64)
 
+        def rotating(shape, dtype, name, tag, bufs):
+            return ring.tile(shape, dtype, name=name, tag=tag, bufs=bufs, align_bytes=64)
+
         def load_list(src, name):
             lst = held([P, src.shape[1]], U16, name)
             nc.sync.dma_start(lst[:], src)
@@ -49,110 +66,103 @@ def tile_list_hop_brew_scores_kernel(
             nc.vector.memset(plane[:].bitcast(I32), 0)
             return plane
 
-        def load_stacked_scales(queue, plane, src):
-            passes = src.shape[0]
-            for q in range(4):
-                rows = src[:, 4 * q : 4 * q + 4, :] if passes > 1 else src[0, 4 * q : 4 * q + 4, :]
-                queue.dma_start(plane[32 * q : 32 * q + 4 * passes, :].bitcast(I32), rows.bitcast(I32))
+        def load_scales(queue, plane, src):
+            for q in range(QUADS):
+                queue.dma_start(plane[32 * q : 32 * q + 4, :].bitcast(I32), src[4 * q : 4 * q + 4, :].bitcast(I32))
 
-        def load_words(src, name):
-            tag, bufs = ("late", 1) if name == "tw1_1" else ("table", 3)
-            words = ring.tile([P, T], U32, name=name, tag=tag, bufs=bufs, align_bytes=64)
+        def load_words(src, name, tag, bufs):
+            words = rotating([P, T], U32, name, tag, bufs)
             nc.sync.dma_start(words[:].bitcast(I32), src.rearrange("p t i -> p (t i)").bitcast(I32))
             return words
 
-        def load_raw(src, name):
-            raw = ring.tile([P, PACK, src.shape[1]], F32, name=name, tag="raw", bufs=4, align_bytes=64)
-            nc.sync.dma_start(raw[:], src.rearrange("(p j) c -> p j c", j=PACK))
-            return raw
-
-        def load_notes(g):
-            rows = ring.tile([P, PACK, M], F32, name="notes%d" % g, tag="table", bufs=3, align_bytes=64)
-            nc.sync.dma_start(rows[:], notes[KP * g : KP * (g + 1), :].rearrange("(p t) m -> p t m", t=PACK))
+        def load_pass(src, name, tag, bufs):
+            rows = rotating([P, PACK, src.shape[1]], F32, name, tag, bufs)
+            nc.sync.dma_start(rows[:], src.rearrange("(p j) c -> p j c", j=PACK))
             return rows
 
-        warm = held([P, 1], F32, "warm")
-        warm_out = held([P, 1], F32, "warm_out")
-        nc.vector.memset(warm[:], 0.0)
-        nc.scalar.activation(warm_out[:], warm[:], ACT.Gelu_apprx_tanh)
-        sc3 = zeroed_plane(T, "sc3")
-        sc2 = zeroed_plane(T, "sc2")
-        sc1 = zeroed_plane(T, "sc1")
-        w2_sc_in = zeroed_plane(H, "w2_sc_in")
-        w4_sc = zeroed_plane(2 * N, "w4_sc")
+        def group(g):
+            return slice(KP * g, KP * (g + 1))
 
-        tw3 = load_words(tab3_words[0], "tw3")
+        def block(t):
+            return slice(P * t, P * (t + 1))
+
+        zero = held([P, 1], F32, "zero")
+        gelu_bias = held([P, 1], F32, "gelu_bias")
+        nc.vector.memset(zero[:], 0.0)
+        nc.scalar.activation(gelu_bias[:], zero[:], ACT.Gelu_apprx_tanh)
+        tab3_sc = zeroed_plane(T, "tab3_sc")
+        tab2_sc = zeroed_plane(T, "tab2_sc")
+        tab1_sc = zeroed_plane(T, "tab1_sc")
+        w2_sc_in = zeroed_plane(H, "w2_sc_in")
+        w4_sc = zeroed_plane(GROUPS * N, "w4_sc")
+
+        tab3_w = load_words(tab3_words[0], "tab3_w", "table", TABLE_BUFS)
         offs3_t = load_list(offs3, "offs3_t")
-        load_stacked_scales(nc.scalar, sc3, tab3_scales)
-        load_stacked_scales(nc.scalar, sc2, tab2_scales)
-        w3_raw = [load_raw(w3[:, 0:KP], "w3_raw0")]
-        b3_t = held([P, 2, PACK], F32, "b3_t")
-        nc.gpsimd.dma_start(b3_t[:], b3.rearrange("(g p t) -> p g t", g=2, t=PACK))
-        load_stacked_scales(nc.gpsimd, sc1, tab_scales)
-        for q in range(4):
+        load_scales(nc.scalar, tab3_sc, tab3_scales[0])
+        load_scales(nc.scalar, tab2_sc, tab2_scales[0])
+        w3_raw = [load_pass(w3[:, group(0)], "w3_raw0", "raw", RAW_BUFS)]
+        b3_t = held([P, GROUPS, PACK], F32, "b3_t")
+        nc.gpsimd.dma_start(b3_t[:], b3.rearrange("(g p t) -> p g t", g=GROUPS, t=PACK))
+        for q in range(QUADS):
+            nc.gpsimd.dma_start(tab1_sc[32 * q : 32 * q + 8, :].bitcast(I32), tab_scales[:, 4 * q : 4 * q + 4, :].bitcast(I32))
+        for q in range(QUADS):
             nc.gpsimd.dma_start(
-                w4_sc[32 * q : 32 * q + 4, :].bitcast(I32).rearrange("r (a n) -> r a n", a=2),
-                w4_scales[:, 4 * q : 4 * q + 4, :].bitcast(I32).rearrange("a r n -> r a n"))
-        w3_raw.append(load_raw(w3[:, KP:H], "w3_raw1"))
+                w4_sc[32 * q : 32 * q + 4, :].bitcast(I32).rearrange("r (g n) -> r g n", g=GROUPS),
+                w4_scales[:, 4 * q : 4 * q + 4, :].bitcast(I32).rearrange("g r n -> r g n"))
+        w3_raw.append(load_pass(w3[:, group(1)], "w3_raw1", "raw", RAW_BUFS))
         offs2_t = load_list(offs2, "offs2_t")
         offs1_t = load_list(offs, "offs1_t")
-        tw2 = load_words(tab2_words[0], "tw2")
+        tab2_w = load_words(tab2_words[0], "tab2_w", "table", TABLE_BUFS)
         pos3_t = load_list(pos3, "pos3_t")
         w2_in = held([P, 2 * H], U8, "w2_in")
         nc.sync.dma_start(w2_in[:].bitcast(I32), w2_words[0].bitcast(I32))
         w1_raw = {}
-        w1_raw[0, 0] = load_raw(w1[0:KP, 0:KP], "w1_raw00")
-        w1_raw[1, 0] = load_raw(w1[KP:K1, 0:KP], "w1_raw10")
-        load_stacked_scales(nc.sync, w2_sc_in, w2_scales)
-        tw1 = [load_words(tab_words[a], "tw1_%d" % a) for a in range(2)]
+        for a in range(2):
+            w1_raw[a, 0] = load_pass(w1[group(a), group(0)], "w1_raw%d0" % a, "raw", RAW_BUFS)
+        load_scales(nc.sync, w2_sc_in, w2_scales[0])
+        tab1_w = [load_words(tab_words[0], "tab1_w0", "table", TABLE_BUFS), load_words(tab_words[1], "tab1_w1", "late", 1)]
         pos1_t = load_list(pos1, "pos1_t")
         pos2_t = load_list(pos2, "pos2_t")
-        s_t, w5_raw = [], []
-        w1_raw[0, 1] = load_raw(w1[0:KP, KP:H], "w1_raw01")
-        w1_raw[1, 1] = load_raw(w1[KP:K1, KP:H], "w1_raw11")
-        s_t.append(load_notes(len(s_t)))
-        s_t.append(load_notes(len(s_t)))
-        w5_raw.append(load_raw(w5[KP * len(w5_raw) : KP * (len(w5_raw) + 1), :], "w5_raw%d" % len(w5_raw)))
-        w5_raw.append(load_raw(w5[KP * len(w5_raw) : KP * (len(w5_raw) + 1), :], "w5_raw%d" % len(w5_raw)))
-        w4_t = held([P, 2, 2 * N], U8, "w4_t")
-        nc.sync.dma_start(w4_t[:].bitcast(I32),
-                          w4_words.bitcast(I32).rearrange("a p n -> p a n"))
+        for a in range(2):
+            w1_raw[a, 1] = load_pass(w1[group(a), group(1)], "w1_raw%d1" % a, "raw", RAW_BUFS)
+        factor = [load_pass(notes[group(g), :], "notes%d" % g, "table", TABLE_BUFS) for g in range(GROUPS)]
+        w5_raw = [load_pass(w5[group(g), :], "w5_raw%d" % g, "raw", RAW_BUFS) for g in range(GROUPS)]
+        w4_t = held([P, GROUPS, 2 * N], U8, "w4_t")
+        nc.sync.dma_start(w4_t[:].bitcast(I32), w4_words.bitcast(I32).rearrange("g p n -> p g n"))
 
-        def gather(window, lst, dtype, name):
+        def gather_table(window, lst, dtype, name):
             picked = held([P, S], dtype, name)
             nc.vector.tensor_copy(picked[:], window[:].indirect(lst[:]))
             return picked
 
-        def staging(width, name):
-            return ring.tile([P, width], BF16, name=name, tag="bf", bufs=3, align_bytes=64)
+        def staging(columns, name):
+            return rotating([P, PACK * columns], BF16, name + "_bf", "stage", STAGE_BUFS)
 
         def quantise(rounded, name, cuts):
-            width = rounded.shape[1] // PACK
-            codes = held([P, width], U32, name + "_codes")
-            scales = held([P, width], U8, name + "_scales")
+            columns = rounded.shape[1] // PACK
+            codes = held([P, columns], U32, name + "_codes")
+            scales = held([P, columns], U8, name + "_scales")
             for c0, c1 in cuts:
                 nc.vector.quantize_mx(out=codes[:, c0:c1].bitcast(E4M3), scales=scales[:, c0:c1],
                                       in_=rounded[:, PACK * c0 : PACK * c1])
             return codes, scales
 
         def quantise_dealt(raw, name):
-            rounded = staging(PACK * KP, name + "_bf")
+            rounded = staging(KP, name)
             nc.scalar.copy(rounded[:].rearrange("p (t m j) -> p m j t", t=PACK, j=PACK),
                            raw[:].rearrange("p j (m t) -> p m j t", t=PACK))
             return quantise(rounded, name, [(0, KP)])
 
-        def quantise_plain(rows, name, cuts):
-            rounded = staging(PACK * rows.shape[2], name + "_bf")
-            copy = nc.vector.tensor_copy if name in GP else nc.scalar.copy
-            copy(rounded[:].rearrange("p (c i j) -> p c j i", i=4, j=PACK),
-                 rows[:].rearrange("p j (c i) -> p c j i", i=4))
+        def quantise_plain(copy, rows, name, cuts):
+            rounded = staging(rows.shape[2], name)
+            copy(rounded[:].rearrange("p (c i j) -> p c j i", i=4, j=PACK), rows[:].rearrange("p j (c i) -> p c j i", i=4))
             return quantise(rounded, name, cuts)
 
         def first_stage(passes, name, bias=None):
-            rows = ring.tile([P, S], F32, name=name, tag="rows", bufs=10, align_bytes=64)
+            rows = rotating([P, S], F32, name, "rows", ROW_BUFS)
             for h in range(S // BANK):
                 cols = slice(BANK * h, BANK * (h + 1))
-                acc = psum.tile([P, BANK], F32, name="acc", tag="acc", bufs=5)
+                acc = psum.tile([P, BANK], F32, name="acc", tag="acc", bufs=ACC_BANKS)
                 for i, (w_codes, w_sc, v_codes, v_sc) in enumerate(passes):
                     nc.tensor.matmul_mx(out=acc[:], lhsT=w_codes, lhsT_scale=w_sc, rhs=v_codes[:, cols].bitcast(E4M3),
                                         rhs_scale=v_sc[:, cols], start=(i == 0), stop=(i == len(passes) - 1))
@@ -162,21 +172,9 @@ def tile_list_hop_brew_scores_kernel(
                     nc.scalar.activation(rows[:, cols], acc[:], ACT.Identity, bias=bias)
             return rows
 
-        def slab(name):
-            if name == "dp1":
-                return ring.tile([P, PACK, M], F32, name=name, tag="late", bufs=1, align_bytes=64)
-            return ring.tile([P, PACK, M], F32, name=name, tag="slab", bufs=2, align_bytes=64)
-
-        v3 = gather(tw3, offs3_t, U32, "v3")
-        v3_sc = gather(sc3, offs3_t, U8, "v3_sc")
-        w3_q = [quantise_dealt(w3_raw[g], "w3_%d" % g) for g in range(2)]
-
-        def tcols(t):
-            return slice(P * t, P * (t + 1))
-
         def d_rows(g, t):
             codes, scales = w3_q[g]
-            return first_stage([(codes[:, tcols(t)].bitcast(E4M3), scales[:, tcols(t)], v3, v3_sc)], "d_rows",
+            return first_stage([(codes[:, block(t)].bitcast(E4M3), scales[:, block(t)], v3, v3_sc)], "d_rows",
                                bias=b3_t[:, g, t : t + 1])
 
         def b_rows(g, t):
@@ -184,114 +182,119 @@ def tile_list_hop_brew_scores_kernel(
             return first_stage([(w2_t[:, 2 * c0 : 2 * (c0 + P)].bitcast(E2M1), w2_sc[:, c0 : c0 + P], v2, v2_sc)], "b_rows")
 
         def a_rows(g, t):
-            return first_stage([(w1_q[a, g][0][:, tcols(t)].bitcast(E4M3), w1_q[a, g][1][:, tcols(t)], v1[a], v1_sc[4 * a :, :])
+            return first_stage([(w1_q[a, g][0][:, block(t)].bitcast(E4M3), w1_q[a, g][1][:, block(t)], v1[a], v1_sc[4 * a :, :])
                                 for a in range(2)], "a_rows")
 
-        def picked_d(g, rows):
-            dp = slab("dp%d" % g)
+        def picked_d(rows, name, tag, bufs):
+            picked = rotating([P, PACK, M], F32, name, tag, bufs)
             for t in range(PACK):
-                nc.vector.tensor_copy(dp[:, t, :], rows[t][:].indirect(pos3_t[:]))
-            return dp
+                nc.vector.tensor_copy(picked[:, t, :], rows[t][:].indirect(pos3_t[:]))
+            return picked
 
+        def picked_b(i):
+            rows = b_rows(*divmod(i, PACK))
+            picked = rotating([P, M], F32, "bp", "bp", PICKED_B_BUFS)
+            nc.vector.tensor_copy(picked[:], rows[:].indirect(pos2_t[:]))
+            return picked
+
+        def picked_a_plus(rows, picked, cols):
+            x = rotating([P, cols.stop - cols.start], F32, "x", "x", SUM_BUFS)
+            nc.vector.tensor_tensor(x[:], rows[:].indirect(pos1_t[:, cols.start // 16 : cols.stop // 16]), picked[:, cols], ALU.add)
+            return x
+
+        def z_quantised(ge_rows, factor_rows, name):
+            columns = ge_rows.shape[2]
+            rounded = staging(columns, name)
+            nc.vector.tensor_tensor(rounded[:].rearrange("p (c i t) -> p c t i", i=2, t=PACK),
+                                    ge_rows.rearrange("p t (c i) -> p c t i", i=2),
+                                    factor_rows.rearrange("p t (c i) -> p c t i", i=2), ALU.mult)
+            return quantise(rounded, name, [(0, columns)])
+
+        v3 = gather_table(tab3_w, offs3_t, U32, "v3")
+        v3_sc = gather_table(tab3_sc, offs3_t, U8, "v3_sc")
+        w3_q = [quantise_dealt(w3_raw[g], "w3_%d" % g) for g in range(GROUPS)]
         d0 = [d_rows(0, t) for t in range(PACK)]
-        v2_sc = gather(sc2, offs2_t, U8, "v2_sc")
-        v2 = gather(tw2, offs2_t, U32, "v2")
+        v2_sc = gather_table(tab2_sc, offs2_t, U8, "v2_sc")
+        v2 = gather_table(tab2_w, offs2_t, U32, "v2")
         w2_t = held([P, 2 * H], U8, "w2_t")
-        nc.vector.tensor_copy(w2_t[:].bitcast(U16).rearrange("p (g t m) -> p g t m", g=2, t=PACK),
-                              w2_in[:].bitcast(U16).rearrange("p (g m t) -> p g t m", g=2, t=PACK))
+        nc.vector.tensor_copy(w2_t[:].bitcast(U16).rearrange("p (g t m) -> p g t m", g=GROUPS, t=PACK),
+                              w2_in[:].bitcast(U16).rearrange("p (g m t) -> p g t m", g=GROUPS, t=PACK))
         w2_sc = held([P, H], U8, "w2_sc")
-        nc.vector.tensor_copy(w2_sc[:].rearrange("p (g t m) -> p g t m", g=2, t=PACK),
-                              w2_sc_in[:].rearrange("p (g m t) -> p g t m", g=2, t=PACK))
-        dp = [picked_d(0, d0)]
+        nc.vector.tensor_copy(w2_sc[:].rearrange("p (g t m) -> p g t m", g=GROUPS, t=PACK),
+                              w2_sc_in[:].rearrange("p (g m t) -> p g t m", g=GROUPS, t=PACK))
+        dp = [picked_d(d0, "dp0", "group", GROUP_BUFS)]
         w1_q = {}
         for a in range(2):
             w1_q[a, 0] = quantise_dealt(w1_raw[a, 0], "w1_%d0" % a)
-        v1_sc = gather(sc1, offs1_t, U8, "v1_sc")
-        v1 = [gather(tw1[a], offs1_t, U32, "v1_%d" % a) for a in range(2)]
+        v1_sc = gather_table(tab1_sc, offs1_t, U8, "v1_sc")
+        v1 = [gather_table(tab1_w[a], offs1_t, U32, "v1_%d" % a) for a in range(2)]
         d1 = [d_rows(1, t) for t in range(PACK)]
-        dp.append(picked_d(1, d1))
+        dp.append(picked_d(d1, "dp1", "late", 1))
 
-        def picked_b(rows, cols):
-            bp = ring.tile([P, cols.stop - cols.start], F32, name="bp", tag="bp", bufs=6, align_bytes=64)
-            nc.vector.tensor_copy(bp[:], rows[:].indirect(pos2_t[:, cols.start // 16 : cols.stop // 16]))
-            return bp
-
-        def picked_sum(rows, bp, cols):
-            x = ring.tile([P, cols.stop - cols.start], F32, name="x", tag="x", bufs=5, align_bytes=64)
-            nc.vector.tensor_tensor(x[:], rows[:].indirect(pos1_t[:, cols.start // 16 : cols.stop // 16]), bp[:, cols], ALU.add)
-            return x
-
-        def add_notes(g):
-            for t in range(PACK):
-                nc.gpsimd.tensor_tensor(s_t[g][:, t, :], dp[g][:, t, :], s_t[g][:, t, :], ALU.add)
-
-        def z_quantised(ge_rows, s_rows, name):
-            rounded = staging(PACK * ge_rows.shape[2], name + "_bf")
-            nc.vector.tensor_tensor(rounded[:].rearrange("p (c i t) -> p c t i", i=4, t=PACK),
-                                    ge_rows.rearrange("p t (c i) -> p c t i", i=4),
-                                    s_rows.rearrange("p t (c i) -> p c t i", i=4), ALU.mult)
-            return quantise(rounded, name, [(0, ge_rows.shape[2])])
-
-        width = M // TAIL
-        b_t = [picked_b(b_rows(0, t), slice(0, M)) for t in range(4)]
-        ge0 = slab("ge0")
-        ge1 = slab("ge1")[:].rearrange("p t m -> p (t m)").rearrange("p (c t m) -> p c t m", c=TAIL, t=PACK)
+        bp = [picked_b(i) for i in range(PACK)]
+        ge0 = rotating([P, PACK, M], F32, "ge0", "group", GROUP_BUFS)
+        ge1 = rotating([P, CHUNKS, PACK, CHUNK], F32, "ge1", "group", GROUP_BUFS)
         y2 = held([P, NT, M], F32, "y2")
-        dq, w5_q, xs = [], [], []
+
+        for g in range(GROUPS):
+            for t in range(PACK):
+                nc.gpsimd.tensor_tensor(factor[g][:, t, :], dp[g][:, t, :], factor[g][:, t, :], ALU.add)
 
         def gelu(i):
-            if i < PACK:
-                nc.scalar.activation(ge0[:, i, :], xs[i][:], ACT.Gelu_apprx_tanh)
-            else:
-                nc.scalar.activation(ge1[:, :, i - PACK, :], xs[i][:].rearrange("p (c m) -> p c m", c=TAIL), ACT.Gelu_apprx_tanh)
-
-        def kettle_scores():
-            for nt in range(NT):
-                acc = psum.tile([P, M], F32, name="y2_acc", tag="y", bufs=3)
-                for g in range(2):
-                    nc.tensor.matmul_mx(out=acc[:], lhsT=w5_q[g][0][:, tcols(nt)].bitcast(E4M3), lhsT_scale=w5_q[g][1][:, tcols(nt)],
-                                        rhs=dq[g][0][:].bitcast(E4M3), rhs_scale=dq[g][1][:], start=(g == 0), stop=(g == 1))
-                nc.scalar.copy(y2[:, nt, :], acc[:])
-
-        add_notes(0)
-        add_notes(1)
-        last = 2 * PACK - 1
-        for i in range(2 * PACK):
             g, t = divmod(i, PACK)
-            if len(b_t) < 2 * PACK and i >= 0:
-                b_t.append(picked_b(b_rows(*divmod(len(b_t), PACK)), slice(0, M)))
-            a_t = a_rows(g, t)
+            if g == 0:
+                nc.scalar.activation(ge0[:, t, :], xs[i][:], ACT.Gelu_apprx_tanh, bias=gelu_bias[:])
+            else:
+                nc.scalar.activation(ge1[:, :, t, :], xs[i][:].rearrange("p (c m) -> p c m", c=CHUNKS),
+                                     ACT.Gelu_apprx_tanh, bias=gelu_bias[:])
+
+        last = TILES - 1
+        dq, w5_q, xs = [], [], []
+        for i in range(TILES):
+            if i + PACK < TILES:
+                bp.append(picked_b(i + PACK))
+            a_t = a_rows(*divmod(i, PACK))
             if i < last:
-                xs.append(picked_sum(a_t, b_t[i], slice(0, M)))
+                xs.append(picked_a_plus(a_t, bp[i], slice(0, M)))
             if i >= LAG:
                 gelu(i - LAG)
-            if i < 2:
-                w1_q[i, 1] = quantise_dealt(w1_raw[i, 1], "w1_%d1" % i)
-            if i == 2:
-                dq.append(quantise_plain(dp[0], "dq0", [(0, M)]))
-            if i == 3:
-                dq.append(quantise_plain(dp[1], "dq1", [(0, M)]))
-            if i in (4, 5):
-                w5_q.append(quantise_plain(w5_raw[len(w5_q)], "w5_%d" % len(w5_q), [(0, 256), (256, N)]))
-            if i == PACK - 1 + LAG:
-                zq0 = z_quantised(ge0[:], s_t[0][:], "zq0")
-        kettle_scores()
-        for i in range(2 * PACK - LAG, last):
+            job, n = divmod(i, 2)
+            if job == 0:
+                w1_q[n, 1] = quantise_dealt(w1_raw[n, 1], "w1_%d1" % n)
+            elif job == 1:
+                dq.append(quantise_plain(nc.scalar.copy, dp[n], "dq%d" % n, [(0, M)]))
+            elif job == 2:
+                w5_q.append(quantise_plain(nc.vector.tensor_copy, w5_raw[n], "w5_%d" % n, W5_CUTS))
+            if i - LAG == PACK - 1:
+                zq0 = z_quantised(ge0[:], factor[0][:], "zq0")
+
+        for nt in range(NT):
+            acc = psum.tile([P, M], F32, name="y2_acc", tag="y2", bufs=Y2_BANKS)
+            for g in range(GROUPS):
+                nc.tensor.matmul_mx(out=acc[:], lhsT=w5_q[g][0][:, block(nt)].bitcast(E4M3), lhsT_scale=w5_q[g][1][:, block(nt)],
+                                    rhs=dq[g][0][:].bitcast(E4M3), rhs_scale=dq[g][1][:], start=(g == 0), stop=(g == GROUPS - 1))
+            nc.scalar.copy(y2[:, nt, :], acc[:])
+        for i in range(TILES - LAG, last):
             gelu(i)
 
-        out_v = out.rearrange("(nt p) m -> p nt m", p=P)
-        for c in range(TAIL):
-            cols = slice(width * c, width * (c + 1))
-            x = picked_sum(a_t, b_t[last], cols)
-            nc.scalar.activation(ge1[:, c, PACK - 1, :], x[:], ACT.Gelu_apprx_tanh)
-            zq1 = z_quantised(ge1[:, c, :, :], s_t[1][:, :, cols], "zq1_%d" % c)
-            acc = psum.tile([P, PACK, width], F32, name="y1_acc", tag="y", bufs=3)
+        y1 = []
+        for c in range(CHUNKS):
+            cols = slice(CHUNK * c, CHUNK * (c + 1))
+            x = picked_a_plus(a_t, bp[last], cols)
+            nc.scalar.activation(ge1[:, c, PACK - 1, :], x[:], ACT.Gelu_apprx_tanh, bias=gelu_bias[:])
+            zq1 = z_quantised(ge1[:, c, :, :], factor[1][:, :, cols], "zq1_%d" % c)
+            z_passes = [(zq0[0][:, cols], zq0[1][:, cols]), (zq1[0][:], zq1[1][:])]
+            acc = psum.tile([P, BANK // CHUNK, CHUNK], F32, name="y1_acc", tag="acc", bufs=ACC_BANKS)
             for nt in range(NT):
-                for g in range(2):
-                    codes, scales = (zq0[0][:, cols], zq0[1][:, cols]) if g == 0 else (zq1[0][:], zq1[1][:])
+                for g, (codes, scales) in enumerate(z_passes):
                     nc.tensor.matmul_mx(out=acc[:, nt, :], lhsT=w4_t[:, g, 2 * P * nt : 2 * P * (nt + 1)].bitcast(E2M1),
                                         lhsT_scale=w4_sc[:, N * g + P * nt : N * g + P * (nt + 1)],
-                                        rhs=codes.bitcast(E4M3), rhs_scale=scales, start=(g == 0), stop=(g == 1))
-            res = held([P, NT, width], F32, "res%d" % c)
+                                        rhs=codes.bitcast(E4M3), rhs_scale=scales, start=(g == 0), stop=(g == GROUPS - 1))
+            y1.append(acc)
+
+        out_v = out.rearrange("(nt p) m -> p nt m", p=P)
+        for c, acc in enumerate(y1):
+            cols = slice(CHUNK * c, CHUNK * (c + 1))
+            res = held([P, NT, CHUNK], F32, "res%d" % c)
             nc.vector.tensor_tensor(res[:], acc[:, 0:NT, :], y2[:, :, cols], ALU.max)
             nc.sync.dma_start(out_v[:, :, cols], res[:])

from contextlib import ExitStack

import concourse.mybir as mybir

K1, K2, K3, T, S, M, H, N = 1024, 512, 512, 2048, 1024, 512, 1024, 384
FLOPS = 2 * H * S * (K1 + K2 + K3) + 2 * 2 * H * N * M

F32 = mybir.dt.float32
BF16 = mybir.dt.bfloat16
I32 = mybir.dt.int32
U32 = mybir.dt.uint32
U16 = mybir.dt.uint16
U8 = mybir.dt.uint8
E4M3 = mybir.dt.float8_e4m3fn_x4
E2M1 = mybir.dt.float4_e2m1fn_x4
ACT = mybir.ActivationFunctionType
ALU = mybir.AluOpType

P = 128
PACK = 4
KP = P * PACK
GROUPS = H // KP
TILES = GROUPS * PACK
QUADS = 4
BANK = 512
NT = N // P
CHUNK = 128
CHUNKS = M // CHUNK
LAG = 3
W5_CUTS = [(0, 256), (256, N)]

TABLE_BUFS = 3
RAW_BUFS = 4
STAGE_BUFS = 3
ROW_BUFS = 10
GROUP_BUFS = 2
PICKED_B_BUFS = PACK + 2
SUM_BUFS = LAG + 2
ACC_BANKS = 5
Y2_BANKS = NT


def tile_list_hop_brew_scores_kernel(
    tc, tab_words, tab_scales, tab2_words, tab2_scales, tab3_words, tab3_scales, offs, offs2, offs3,
    pos1, pos2, pos3, w1, w2_words, w2_scales, w3, b3, notes, w4_words, w4_scales, w5, out,
):
    nc = tc.nc
    with ExitStack() as ctx:
        keep = ctx.enter_context(tc.tile_pool(name="keep", bufs=1))
        ring = ctx.enter_context(tc.tile_pool(name="ring", bufs=1))
        psum = ctx.enter_context(tc.psum_pool(name="psum", bufs=1))

        def held(shape, dtype, name):
            return keep.tile(shape, dtype, name=name, align_bytes=64)

        def rotating(shape, dtype, name, tag, bufs):
            return ring.tile(shape, dtype, name=name, tag=tag, bufs=bufs, align_bytes=64)

        def load_list(src, name):
            lst = held([P, src.shape[1]], U16, name)
            nc.sync.dma_start(lst[:], src)
            return lst

        def zeroed_plane(width, name):
            plane = held([P, width], U8, name)
            nc.vector.memset(plane[:].bitcast(I32), 0)
            return plane

        def load_scales(queue, plane, src):
            for q in range(QUADS):
                queue.dma_start(plane[32 * q : 32 * q + 4, :].bitcast(I32), src[4 * q : 4 * q + 4, :].bitcast(I32))

        def load_words(src, name, tag, bufs):
            words = rotating([P, T], U32, name, tag, bufs)
            nc.sync.dma_start(words[:].bitcast(I32), src.rearrange("p t i -> p (t i)").bitcast(I32))
            return words

        def load_pass(src, name, tag, bufs):
            rows = rotating([P, PACK, src.shape[1]], F32, name, tag, bufs)
            nc.sync.dma_start(rows[:], src.rearrange("(p j) c -> p j c", j=PACK))
            return rows

        def group(g):
            return slice(KP * g, KP * (g + 1))

        def block(t):
            return slice(P * t, P * (t + 1))

        zero = held([P, 1], F32, "zero")
        gelu_bias = held([P, 1], F32, "gelu_bias")
        nc.vector.memset(zero[:], 0.0)
        nc.scalar.activation(gelu_bias[:], zero[:], ACT.Gelu_apprx_tanh)
        tab3_sc = zeroed_plane(T, "tab3_sc")
        tab2_sc = zeroed_plane(T, "tab2_sc")
        tab1_sc = zeroed_plane(T, "tab1_sc")
        w2_sc_in = zeroed_plane(H, "w2_sc_in")
        w4_sc = zeroed_plane(GROUPS * N, "w4_sc")

        tab3_w = load_words(tab3_words[0], "tab3_w", "table", TABLE_BUFS)
        offs3_t = load_list(offs3, "offs3_t")
        load_scales(nc.scalar, tab3_sc, tab3_scales[0])
        load_scales(nc.scalar, tab2_sc, tab2_scales[0])
        w3_raw = [load_pass(w3[:, group(0)], "w3_raw0", "raw", RAW_BUFS)]
        b3_t = held([P, GROUPS, PACK], F32, "b3_t")
        nc.gpsimd.dma_start(b3_t[:], b3.rearrange("(g p t) -> p g t", g=GROUPS, t=PACK))
        for q in range(QUADS):
            nc.gpsimd.dma_start(tab1_sc[32 * q : 32 * q + 8, :].bitcast(I32), tab_scales[:, 4 * q : 4 * q + 4, :].bitcast(I32))
        for q in range(QUADS):
            nc.gpsimd.dma_start(
                w4_sc[32 * q : 32 * q + 4, :].bitcast(I32).rearrange("r (g n) -> r g n", g=GROUPS),
                w4_scales[:, 4 * q : 4 * q + 4, :].bitcast(I32).rearrange("g r n -> r g n"))
        w3_raw.append(load_pass(w3[:, group(1)], "w3_raw1", "raw", RAW_BUFS))
        offs2_t = load_list(offs2, "offs2_t")
        offs1_t = load_list(offs, "offs1_t")
        tab2_w = load_words(tab2_words[0], "tab2_w", "table", TABLE_BUFS)
        pos3_t = load_list(pos3, "pos3_t")
        w2_in = held([P, 2 * H], U8, "w2_in")
        nc.sync.dma_start(w2_in[:].bitcast(I32), w2_words[0].bitcast(I32))
        w1_raw = {}
        for a in range(2):
            w1_raw[a, 0] = load_pass(w1[group(a), group(0)], "w1_raw%d0" % a, "raw", RAW_BUFS)
        load_scales(nc.sync, w2_sc_in, w2_scales[0])
        tab1_w = [load_words(tab_words[0], "tab1_w0", "table", TABLE_BUFS), load_words(tab_words[1], "tab1_w1", "late", 1)]
        pos1_t = load_list(pos1, "pos1_t")
        pos2_t = load_list(pos2, "pos2_t")
        for a in range(2):
            w1_raw[a, 1] = load_pass(w1[group(a), group(1)], "w1_raw%d1" % a, "raw", RAW_BUFS)
        factor = [load_pass(notes[group(g), :], "notes%d" % g, "table", TABLE_BUFS) for g in range(GROUPS)]
        w5_raw = [load_pass(w5[group(g), :], "w5_raw%d" % g, "raw", RAW_BUFS) for g in range(GROUPS)]
        w4_t = held([P, GROUPS, 2 * N], U8, "w4_t")
        nc.sync.dma_start(w4_t[:].bitcast(I32), w4_words.bitcast(I32).rearrange("g p n -> p g n"))

        def gather_table(window, lst, dtype, name):
            picked = held([P, S], dtype, name)
            nc.vector.tensor_copy(picked[:], window[:].indirect(lst[:]))
            return picked

        def staging(columns, name):
            return rotating([P, PACK * columns], BF16, name + "_bf", "stage", STAGE_BUFS)

        def quantise(rounded, name, cuts):
            columns = rounded.shape[1] // PACK
            codes = held([P, columns], U32, name + "_codes")
            scales = held([P, columns], U8, name + "_scales")
            for c0, c1 in cuts:
                nc.vector.quantize_mx(out=codes[:, c0:c1].bitcast(E4M3), scales=scales[:, c0:c1],
                                      in_=rounded[:, PACK * c0 : PACK * c1])
            return codes, scales

        def quantise_dealt(raw, name):
            rounded = staging(KP, name)
            nc.scalar.copy(rounded[:].rearrange("p (t m j) -> p m j t", t=PACK, j=PACK),
                           raw[:].rearrange("p j (m t) -> p m j t", t=PACK))
            return quantise(rounded, name, [(0, KP)])

        def quantise_plain(copy, rows, name, cuts):
            rounded = staging(rows.shape[2], name)
            copy(rounded[:].rearrange("p (c i j) -> p c j i", i=4, j=PACK), rows[:].rearrange("p j (c i) -> p c j i", i=4))
            return quantise(rounded, name, cuts)

        def first_stage(passes, name, bias=None):
            rows = rotating([P, S], F32, name, "rows", ROW_BUFS)
            for h in range(S // BANK):
                cols = slice(BANK * h, BANK * (h + 1))
                acc = psum.tile([P, BANK], F32, name="acc", tag="acc", bufs=ACC_BANKS)
                for i, (w_codes, w_sc, v_codes, v_sc) in enumerate(passes):
                    nc.tensor.matmul_mx(out=acc[:], lhsT=w_codes, lhsT_scale=w_sc, rhs=v_codes[:, cols].bitcast(E4M3),
                                        rhs_scale=v_sc[:, cols], start=(i == 0), stop=(i == len(passes) - 1))
                if bias is None:
                    nc.scalar.copy(rows[:, cols], acc[:])
                else:
                    nc.scalar.activation(rows[:, cols], acc[:], ACT.Identity, bias=bias)
            return rows

        def d_rows(g, t):
            codes, scales = w3_q[g]
            return first_stage([(codes[:, block(t)].bitcast(E4M3), scales[:, block(t)], v3, v3_sc)], "d_rows",
                               bias=b3_t[:, g, t : t + 1])

        def b_rows(g, t):
            c0 = KP * g + P * t
            return first_stage([(w2_t[:, 2 * c0 : 2 * (c0 + P)].bitcast(E2M1), w2_sc[:, c0 : c0 + P], v2, v2_sc)], "b_rows")

        def a_rows(g, t):
            return first_stage([(w1_q[a, g][0][:, block(t)].bitcast(E4M3), w1_q[a, g][1][:, block(t)], v1[a], v1_sc[4 * a :, :])
                                for a in range(2)], "a_rows")

        def picked_d(rows, name, tag, bufs):
            picked = rotating([P, PACK, M], F32, name, tag, bufs)
            for t in range(PACK):
                nc.vector.tensor_copy(picked[:, t, :], rows[t][:].indirect(pos3_t[:]))
            return picked

        def picked_b(i):
            rows = b_rows(*divmod(i, PACK))
            picked = rotating([P, M], F32, "bp", "bp", PICKED_B_BUFS)
            nc.vector.tensor_copy(picked[:], rows[:].indirect(pos2_t[:]))
            return picked

        def picked_a_plus(rows, picked, cols):
            x = rotating([P, cols.stop - cols.start], F32, "x", "x", SUM_BUFS)
            nc.vector.tensor_tensor(x[:], rows[:].indirect(pos1_t[:, cols.start // 16 : cols.stop // 16]), picked[:, cols], ALU.add)
            return x

        def z_quantised(ge_rows, factor_rows, name):
            columns = ge_rows.shape[2]
            rounded = staging(columns, name)
            nc.vector.tensor_tensor(rounded[:].rearrange("p (c i t) -> p c t i", i=2, t=PACK),
                                    ge_rows.rearrange("p t (c i) -> p c t i", i=2),
                                    factor_rows.rearrange("p t (c i) -> p c t i", i=2), ALU.mult)
            return quantise(rounded, name, [(0, columns)])

        v3 = gather_table(tab3_w, offs3_t, U32, "v3")
        v3_sc = gather_table(tab3_sc, offs3_t, U8, "v3_sc")
        w3_q = [quantise_dealt(w3_raw[g], "w3_%d" % g) for g in range(GROUPS)]
        d0 = [d_rows(0, t) for t in range(PACK)]
        v2_sc = gather_table(tab2_sc, offs2_t, U8, "v2_sc")
        v2 = gather_table(tab2_w, offs2_t, U32, "v2")
        w2_t = held([P, 2 * H], U8, "w2_t")
        nc.vector.tensor_copy(w2_t[:].bitcast(U16).rearrange("p (g t m) -> p g t m", g=GROUPS, t=PACK),
                              w2_in[:].bitcast(U16).rearrange("p (g m t) -> p g t m", g=GROUPS, t=PACK))
        w2_sc = held([P, H], U8, "w2_sc")
        nc.vector.tensor_copy(w2_sc[:].rearrange("p (g t m) -> p g t m", g=GROUPS, t=PACK),
                              w2_sc_in[:].rearrange("p (g m t) -> p g t m", g=GROUPS, t=PACK))
        dp = [picked_d(d0, "dp0", "group", GROUP_BUFS)]
        w1_q = {}
        for a in range(2):
            w1_q[a, 0] = quantise_dealt(w1_raw[a, 0], "w1_%d0" % a)
        v1_sc = gather_table(tab1_sc, offs1_t, U8, "v1_sc")
        v1 = [gather_table(tab1_w[a], offs1_t, U32, "v1_%d" % a) for a in range(2)]
        d1 = [d_rows(1, t) for t in range(PACK)]
        dp.append(picked_d(d1, "dp1", "late", 1))

        bp = [picked_b(i) for i in range(PACK)]
        ge0 = rotating([P, PACK, M], F32, "ge0", "group", GROUP_BUFS)
        ge1 = rotating([P, CHUNKS, PACK, CHUNK], F32, "ge1", "group", GROUP_BUFS)
        y2 = held([P, NT, M], F32, "y2")

        for g in range(GROUPS):
            for t in range(PACK):
                nc.gpsimd.tensor_tensor(factor[g][:, t, :], dp[g][:, t, :], factor[g][:, t, :], ALU.add)

        def gelu(i):
            g, t = divmod(i, PACK)
            if g == 0:
                nc.scalar.activation(ge0[:, t, :], xs[i][:], ACT.Gelu_apprx_tanh, bias=gelu_bias[:])
            else:
                nc.scalar.activation(ge1[:, :, t, :], xs[i][:].rearrange("p (c m) -> p c m", c=CHUNKS),
                                     ACT.Gelu_apprx_tanh, bias=gelu_bias[:])

        last = TILES - 1
        dq, w5_q, xs = [], [], []
        for i in range(TILES):
            if i + PACK < TILES:
                bp.append(picked_b(i + PACK))
            a_t = a_rows(*divmod(i, PACK))
            if i < last:
                xs.append(picked_a_plus(a_t, bp[i], slice(0, M)))
            if i >= LAG:
                gelu(i - LAG)
            job, n = divmod(i, 2)
            if job == 0:
                w1_q[n, 1] = quantise_dealt(w1_raw[n, 1], "w1_%d1" % n)
            elif job == 1:
                dq.append(quantise_plain(nc.scalar.copy, dp[n], "dq%d" % n, [(0, M)]))
            elif job == 2:
                w5_q.append(quantise_plain(nc.vector.tensor_copy, w5_raw[n], "w5_%d" % n, W5_CUTS))
            if i - LAG == PACK - 1:
                zq0 = z_quantised(ge0[:], factor[0][:], "zq0")

        for nt in range(NT):
            acc = psum.tile([P, M], F32, name="y2_acc", tag="y2", bufs=Y2_BANKS)
            for g in range(GROUPS):
                nc.tensor.matmul_mx(out=acc[:], lhsT=w5_q[g][0][:, block(nt)].bitcast(E4M3), lhsT_scale=w5_q[g][1][:, block(nt)],
                                    rhs=dq[g][0][:].bitcast(E4M3), rhs_scale=dq[g][1][:], start=(g == 0), stop=(g == GROUPS - 1))
            nc.scalar.copy(y2[:, nt, :], acc[:])
        for i in range(TILES - LAG, last):
            gelu(i)

        y1 = []
        for c in range(CHUNKS):
            cols = slice(CHUNK * c, CHUNK * (c + 1))
            x = picked_a_plus(a_t, bp[last], cols)
            nc.scalar.activation(ge1[:, c, PACK - 1, :], x[:], ACT.Gelu_apprx_tanh, bias=gelu_bias[:])
            zq1 = z_quantised(ge1[:, c, :, :], factor[1][:, :, cols], "zq1_%d" % c)
            z_passes = [(zq0[0][:, cols], zq0[1][:, cols]), (zq1[0][:], zq1[1][:])]
            acc = psum.tile([P, BANK // CHUNK, CHUNK], F32, name="y1_acc", tag="acc", bufs=ACC_BANKS)
            for nt in range(NT):
                for g, (codes, scales) in enumerate(z_passes):
                    nc.tensor.matmul_mx(out=acc[:, nt, :], lhsT=w4_t[:, g, 2 * P * nt : 2 * P * (nt + 1)].bitcast(E2M1),
                                        lhsT_scale=w4_sc[:, N * g + P * nt : N * g + P * (nt + 1)],
                                        rhs=codes.bitcast(E4M3), rhs_scale=scales, start=(g == 0), stop=(g == GROUPS - 1))
            y1.append(acc)

        out_v = out.rearrange("(nt p) m -> p nt m", p=P)
        for c, acc in enumerate(y1):
            cols = slice(CHUNK * c, CHUNK * (c + 1))
            res = held([P, NT, CHUNK], F32, "res%d" % c)
            nc.vector.tensor_tensor(res[:], acc[:, 0:NT, :], y2[:, :, cols], ALU.max)
            nc.sync.dma_start(out_v[:, :, cols], res[:])
